import numpy as np
import ml_dtypes


def mxq(x, axis, fmt="e4m3"):
    dtype, down = {"e4m3": (ml_dtypes.float8_e4m3fn, 7), "e5m2": (ml_dtypes.float8_e5m2, 14)}[fmt]
    v = np.moveaxis(np.asarray(x, np.float32).astype(ml_dtypes.bfloat16).astype(np.float64), axis, -1)
    blocks = v.reshape(v.shape[:-1] + (-1, 32))
    amax = np.abs(blocks).max(-1, keepdims=True)
    byte = np.maximum(np.where(amax > 0, np.frexp(amax)[1] - 1 + 127, 0) - down, 1)
    scale = np.exp2(byte - 127.0)
    codes = (blocks / scale).astype(np.float32).astype(dtype).astype(np.float64)
    return np.moveaxis((codes * scale).reshape(v.shape), -1, axis)


WIDE = False


def mx_kscale(k):
    if not WIDE:
        return np.ones(k)
    levels = np.array([10, -10, 5, -5, 0])
    if k % 512:
        return np.exp2(np.random.permutation(np.resize(levels, k // 32))).repeat(32)
    a = np.empty((k // 512, 16))
    for p in range(k // 512):
        a[p, :8] = np.random.permutation(np.resize(levels, 8))
        for g in range(8):
            far = levels[np.abs(levels - a[p, g]) >= 10]
            a[p, g + 8] = far[np.random.randint(len(far))]
    return np.exp2(a.ravel()).repeat(32)


BF16 = ml_dtypes.bfloat16


def bf(x):
    return np.asarray(x, np.float32).astype(BF16)


def f64(x):
    return np.asarray(x).astype(np.float64)


E2M1 = np.array([0.0, 0.5, 1.0, 1.5, 2.0, 3.0, 4.0, 6.0, -0.0, -0.5, -1.0, -1.5, -2.0, -3.0, -4.0, -6.0])


def pack_weight(w, fmt):
    k, n = w.shape
    w = f64(bf(w)).reshape(k // 32, 32, n)
    amax = np.abs(w).max(1)
    if fmt == "e4m3":
        byte = np.frexp(amax)[1] - 1 + 127 - 7
    else:
        mant, ex = np.frexp(amax / 6.0)
        byte = np.where(mant > 0.5, ex, ex - 1) + 127
    byte = np.clip(np.where(amax > 0, byte, 1), 1, 254)
    scaled = (w * np.exp2(127.0 - byte)[:, None, :]).reshape(k, n).astype(np.float32)
    by_word = np.ascontiguousarray(scaled.reshape(k // 512, 128, 4, n).transpose(0, 1, 3, 2))
    if fmt == "e4m3":
        words = by_word.astype(ml_dtypes.float8_e4m3fn).view(np.uint8)
    else:
        c = by_word.astype(ml_dtypes.float4_e2m1fn).view(np.uint8) & 0xF
        words = c[..., 0::2] | (c[..., 1::2] << 4)
    return np.ascontiguousarray(words), np.ascontiguousarray(byte.astype(np.uint8).reshape(k // 512, 16, n))


def unpack_weight(words, scales, fmt):
    g, p, n, _ = words.shape
    if fmt == "e4m3":
        vals = np.ascontiguousarray(words).view(ml_dtypes.float8_e4m3fn).astype(np.float64)
    else:
        nib = np.empty((g, p, n, 4), np.uint8)
        nib[..., 0::2] = words & 0xF
        nib[..., 1::2] = words >> 4
        vals = E2M1[nib]
    vals = vals * np.repeat(np.exp2(scales.astype(np.float64) - 127.0), 8, axis=1)[..., None]
    return vals.transpose(0, 1, 3, 2).reshape(g * 512, n)
def pack4(w):
    words, scales = pack_weight(w, "e2m1")
    return words.reshape(words.shape[0], 128, -1), scales


def unpack4(words, scales):
    return unpack_weight(words.reshape(words.shape[0], 128, -1, 2), scales, "e2m1")


def planes(Y):
    n, m = Y.shape
    b = f64(bf(Y)).reshape(n // 32, 32, m)
    amax = np.abs(b).max(1)
    byte = np.clip(np.where(amax > 0, np.frexp(amax)[1] - 1 + 127 - 7, 1), 1, 254)
    codes = (b * np.exp2(127.0 - byte)[:, None, :]).reshape(n, m).astype(np.float32).astype(ml_dtypes.float8_e4m3fn).view(np.uint8)
    words = codes.reshape(n // 512, 128, 4, m).transpose(0, 1, 3, 2)
    return np.ascontiguousarray(words), np.ascontiguousarray(byte.astype(np.uint8).reshape(n // 512, 16, m))


B, N = 1024, 1536

def setup_inputs():
    s = mx_kscale(N)
    h = np.exp(0.8 * np.random.randn(N))
    upper = np.triu(np.random.randn(N, N), 1)
    adj = np.exp(1.5 * (upper + upper.T)) * h[:, None] * h[None, :] * (1.0 - np.eye(N))
    adj = adj / adj.sum(axis=1).mean()
    deg = adj.sum(axis=1)
    inv_root = 1.0 / np.sqrt(deg)
    w_words, w_scales = pack4(adj * inv_root[None, :] * s[:, None])
    amp = np.exp(0.7 * np.random.randn(N))
    x = amp[None, :] * (np.random.randn(B, 1) + np.random.randn(B, N))
    tau = 0.15 * np.exp(0.3 * np.random.randn(N))
    return {"x": bf(x), "r": bf(inv_root / s), "w_words": w_words, "w_scales": w_scales, "tau": bf(tau)}

def reference(x, r, w_words, w_scales, tau):
    x, r, tau = f64(x), f64(r), f64(tau)
    W = unpack4(w_words, w_scales)
    u = mxq(x * r[None, :], 1, "e4m3")
    z = x - (u @ W)
    y = z - np.maximum(np.minimum(z, tau[None, :]), -tau[None, :])
    Y = y.T
    words, scales = planes(Y)
    return y, words, scales

@@ -1,0 +1,248 @@
+from contextlib import ExitStack
+
+import concourse.mybir as mybir
+from concourse.masks import make_identity
+
+B, N = 1024, 1536
+FLOPS = 2 * B * N * N
+
+F32 = mybir.dt.float32
+BF16 = mybir.dt.bfloat16
+I32 = mybir.dt.int32
+U32 = mybir.dt.uint32
+U8 = mybir.dt.uint8
+FP8X4 = mybir.dt.float8_e4m3fn_x4
+FP4X4 = mybir.dt.float4_e2m1fn_x4
+ALU = mybir.AluOpType
+ACT = mybir.ActivationFunctionType
+
+P = 128
+GROUP = 512
+GROUPS = N // GROUP
+BLOCK = 256
+TILES = BLOCK // P
+BLOCKS = B // BLOCK
+STEPS = BLOCKS * GROUPS
+
+
+def tile_soft_thresholded_graph_laplacian_g4_kernel(tc, x, r, w_words, w_scales, tau, out_0, out_1, out_2):
+    nc = tc.nc
+    with ExitStack() as ctx:
+        keep = ctx.enter_context(tc.tile_pool(name="keep", bufs=1))
+        work = ctx.enter_context(tc.tile_pool(name="work", bufs=3))
+        psum = ctx.enter_context(tc.psum_pool(name="psum", bufs=2))
+        ctx.enter_context(tc.manual_schedule())
+
+        ident = keep.tile([P, P], F32, name="ident")
+        make_identity(nc, ident[:])
+        w_scale = keep.tile([P, GROUPS, N], U8, name="w_scale", align_bytes=64)
+        nc.vector.memset(w_scale[:].rearrange("p g n -> p (g n)").bitcast(I32), 0)
+
+        raw = {}
+
+        def load_x(h, k0, k1, name):
+            t = keep.tile([P, TILES, (k1 - k0) * GROUP], BF16, name=name)
+            src = x[h * BLOCK:(h + 1) * BLOCK, k0 * GROUP:k1 * GROUP].rearrange("(i p) n -> p i n", p=P)
+            nc.sync.dma_start(out=t[:], in_=src)
+            for k in range(k0, k1):
+                raw[h * GROUPS + k] = t[:, :, (k - k0) * GROUP:(k - k0 + 1) * GROUP]
+
+        w_code = {}
+
+        def load_w(g):
+            t = keep.tile([P, GROUPS, 2 * GROUP], U8, name="w_code%d" % g, align_bytes=64)
+            src = w_words[:, :, 2 * GROUP * g:2 * GROUP * (g + 1)].bitcast(I32).rearrange("k p n -> p k n")
+            nc.sync.dma_start(out=t[:].bitcast(I32), in_=src)
+            w_code[g] = t
+
+        r_sb = keep.tile([P, GROUPS, 4], BF16, name="r_sb")
+        tau_sb = keep.tile([P, GROUPS, 4], BF16, name="tau_sb")
+        load_x(0, 0, 1, "x_first")
+        nc.scalar.dma_start(out=r_sb[:], in_=r.rearrange("(g p t) -> p g t", p=P, t=4))
+        load_x(0, 1, GROUPS, "x_rest")
+        load_w(0)
+        for q in range(4):
+            nc.scalar.dma_start(
+                out=w_scale[32 * q:32 * q + 4, :, :].bitcast(I32),
+                in_=w_scales[:, 4 * q:4 * q + 4, :].bitcast(I32).rearrange("k r n -> r k n"),
+            )
+        nc.sync.dma_start(out=tau_sb[:], in_=tau.rearrange("(g p t) -> p g t", p=P, t=4))
+        load_x(1, 0, GROUPS, "x_1")
+        load_w(1)
+        load_w(2)
+        load_x(2, 0, GROUPS, "x_2")
+        load_x(3, 0, GROUPS, "x_3")
+
+        tau_pos = keep.tile([P, GROUPS * 4], F32, name="tau_pos")
+        tau_neg = keep.tile([P, GROUPS * 4], F32, name="tau_neg")
+        tau_flat = tau_sb[:].rearrange("p g t -> p (g t)")
+        nc.gpsimd.tensor_scalar(tau_pos[:], tau_flat, 1.0, 0.0, ALU.mult, ALU.add)
+        nc.scalar.activation(out=tau_neg[:], in_=tau_flat, func=ACT.Copy, scale=-1.0)
+
+        xs, xt, ub, uq, us = {}, {}, {}, {}, {}
+        zs, zt, yt, yb, ya, acc = {}, {}, {}, {}, {}, {}
+        y_scale = [keep.tile([P, GROUPS, 2 * BLOCK], U8, name="y_scale%d" % i, align_bytes=64) for i in range(BLOCKS // 2)]
+
+        def sort_x(n):
+            xs[n] = keep.tile([P, TILES, 2, P], F32, name="xs%d" % n)
+            nc.scalar.copy(out=xs[n][:], in_=raw[n].bitcast(F32).rearrange("b i (p u) -> b i u p", u=2))
+
+        def turn_x(n):
+            xt[n] = psum.tile([P, 2, TILES, P], F32, name="xt")
+            for i in range(TILES):
+                for u in range(2):
+                    if n < GROUPS:
+                        src = raw[n].bitcast(F32)[:, i, u::2]
+                    else:
+                        src = xs[n][:, i, u, :]
+                    nc.tensor.transpose(xt[n][:, u, i, :], src, ident[:])
+
+        def scale_x(n):
+            ub[n] = work.tile([P, BLOCK, 2, 2], BF16, name="ub", align_bytes=64)
+            src = xt[n][:].rearrange("p u i b -> p (u i b)").bitcast(BF16).rearrange("p (u m e) -> p m u e", u=2, e=2)
+            fac = r_sb[:, n % GROUPS, :].rearrange("p (u e) -> p u e", u=2).unsqueeze(1).to_broadcast([P, BLOCK, 2, 2])
+            nc.vector.tensor_tensor(out=ub[n][:], in0=src, in1=fac, op=ALU.mult)
+
+        def quant_u(n):
+            uq[n] = keep.tile([P, BLOCK], U32, name="uq%d" % n, align_bytes=64)
+            us[n] = keep.tile([P, BLOCK], U8, name="us%d" % n, align_bytes=64)
+            nc.vector.quantize_mx(out=uq[n][:].bitcast(FP8X4), scales=us[n][:], in_=ub[n][:].rearrange("p m u e -> p (m u e)"))
+
+        def product(s):
+            h, g = divmod(s, GROUPS)
+            acc[s] = [psum.tile([P, GROUP], F32, name="acc") for i in range(TILES)]
+            order = [(i, k) for i in range(TILES) for k in range(GROUPS)]
+            if s == 0:
+                order = [(i, k) for k in range(GROUPS) for i in range(TILES)]
+            for i, k in order:
+                n = h * GROUPS + k
+                nc.tensor.matmul_mx(
+                    out=acc[s][i][:],
+                    lhsT=uq[n][:, i * P:(i + 1) * P].bitcast(FP8X4),
+                    lhsT_scale=us[n][:, i * P:(i + 1) * P],
+                    rhs=w_code[g][:, k, :].bitcast(FP4X4),
+                    rhs_scale=w_scale[:, k, g * GROUP:(g + 1) * GROUP],
+                    start=(k == 0),
+                    stop=(k == GROUPS - 1),
+                )
+
+        def difference(s):
+            zs[s] = []
+            for i in range(TILES):
+                z = work.tile([P, 2, 2, P], F32, name="zs", bufs=2 * TILES + 1)
+                xv = xs[s][:, i, :, :].rearrange("b u p -> b (u p)").bitcast(BF16).rearrange("b (u p e) -> b u e p", u=2, e=2)
+                av = acc[s][i][:].rearrange("b (p u e) -> b u e p", u=2, e=2)
+                nc.vector.tensor_tensor(out=z[:], in0=xv, in1=av, op=ALU.subtract)
+                zs[s].append(z)
+
+        def turn_z(s):
+            zt[s] = [psum.tile([P, 2, TILES, P], F32, name="zt") for u in range(2)]
+            for u in range(2):
+                for e in range(2):
+                    for i in range(TILES):
+                        nc.tensor.transpose(zt[s][u][:, e, i, :], zs[s][i][:, u, e, :], ident[:])
+
+        def threshold(s):
+            g = s % GROUPS
+            yt[s] = work.tile([P, 4, BLOCK], F32, name="yt")
+            for u in range(2):
+                above = work.tile([P, 2, BLOCK], F32, name="above")
+                for e in range(2):
+                    c = 4 * g + 2 * u + e
+                    zv = zt[s][u][:, e, :, :].rearrange("p i b -> p (i b)")
+                    nc.scalar.activation(out=above[:, e, :], in_=zv, func=ACT.Relu, bias=tau_neg[:, c:c + 1])
+                for e in range(2):
+                    c = 4 * g + 2 * u + e
+                    zv = zt[s][u][:, e, :, :].rearrange("p i b -> p (i b)")
+                    nc.vector.scalar_tensor_tensor(
+                        out=yt[s][:, 2 * u + e, :], in0=zv, scalar=tau_pos[:, c:c + 1], in1=above[:, e, :], op0=ALU.add, op1=ALU.min
+                    )
+
+        def round_y(s):
+            yb[s] = work.tile([P, BLOCK, 4], BF16, name="yb", align_bytes=64)
+            src = yt[s][:].rearrange("p t m -> p m t")
+            if s == STEPS - 1:
+                nc.vector.tensor_copy(out=yb[s][:], in_=src)
+            else:
+                nc.gpsimd.tensor_scalar(yb[s][:], src, 1.0, -0.0, ALU.mult, ALU.add)
+
+        def quant_y(s):
+            h, g = divmod(s, GROUPS)
+            codes = work.tile([P, BLOCK], U32, name="codes", align_bytes=64)
+            plane = y_scale[h // 2]
+            nc.vector.quantize_mx(
+                out=codes[:].bitcast(FP8X4),
+                scales=plane[:, g, (h % 2) * BLOCK:(h % 2 + 1) * BLOCK],
+                in_=yb[s][:].rearrange("p m t -> p (m t)"),
+            )
+            dst = out_1[g, :, h * BLOCK:(h + 1) * BLOCK, :].rearrange("p m t -> p (m t)").bitcast(I32)
+            nc.sync.dma_start(out=dst, in_=codes[:].bitcast(I32))
+            if s % (2 * GROUPS) == 2 * GROUPS - 1:
+                cols = slice((h // 2) * 2 * BLOCK, (h // 2 + 1) * 2 * BLOCK)
+                for q in range(4):
+                    nc.sync.dma_start(
+                        out=out_2[:, 4 * q:4 * q + 4, cols].bitcast(I32).rearrange("g r m -> r g m"),
+                        in_=plane[32 * q:32 * q + 4, :, :].bitcast(I32),
+                    )
+
+        def turn_y(s):
+            ya[s] = [psum.tile([P, 4, P], F32, name="ya") for i in range(TILES)]
+            for i in range(TILES):
+                for t in range(4):
+                    nc.tensor.transpose(ya[s][i][:, t, :], yt[s][:, t, i * P:(i + 1) * P], ident[:])
+
+        def store_y(s):
+            h, g = divmod(s, GROUPS)
+            for i in range(TILES):
+                rows = work.tile([P, P, 4], F32, name="rows", bufs=4)
+                src = ya[s][i][:].rearrange("b t p -> b p t")
+                if s == STEPS - 1 and i == TILES - 1:
+                    nc.vector.tensor_copy(out=rows[:], in_=src)
+                else:
+                    nc.scalar.copy(out=rows[:], in_=src)
+                b0 = h * BLOCK + i * P
+                nc.sync.dma_start(out=out_0[b0:b0 + P, g * GROUP:(g + 1) * GROUP], in_=rows[:].rearrange("b p t -> b (p t)"))
+
+        turn_x(0)
+        turn_x(1)
+        scale_x(0)
+        turn_x(2)
+        scale_x(1)
+        quant_u(0)
+        scale_x(2)
+        quant_u(1)
+        quant_u(2)
+        for n in range(GROUPS):
+            sort_x(n)
+
+        def turned_at(s):
+            if s == 0:
+                return [GROUPS, GROUPS + 1]
+            return [s + GROUPS + 1] if 0 < s < STEPS - GROUPS - 1 else []
+
+        for s in range(STEPS + 2):
+            if s < STEPS:
+                product(s)
+            for n in turned_at(s - 1):
+                scale_x(n)
+            if s < STEPS:
+                difference(s)
+            for n in turned_at(s - 1):
+                quant_u(n)
+            if 2 <= s <= STEPS:
+                quant_y(s - 2)
+            for n in turned_at(s):
+                sort_x(n)
+            if 1 <= s <= STEPS:
+                turn_z(s - 1)
+            if s >= 2:
+                turn_y(s - 2)
+            for n in turned_at(s):
+                turn_x(n)
+            if 1 <= s <= STEPS:
+                threshold(s - 1)
+                round_y(s - 1)
+            if s == STEPS + 1:
+                quant_y(s - 2)
+            if s >= 2:
+                store_y(s - 2)

@@ -69,8 +69,8 @@ def tile_soft_thresholded_graph_laplacian_g4_kernel(tc, x, r, w_words, w_scales,
         nc.sync.dma_start(out=tau_sb[:], in_=tau.rearrange("(g p t) -> p g t", p=P, t=4))
         load_x(1, 0, GROUPS, "x_1")
         load_w(1)
-        load_w(2)
         load_x(2, 0, GROUPS, "x_2")
+        load_w(2)
         load_x(3, 0, GROUPS, "x_3")
 
         tau_pos = keep.tile([P, GROUPS * 4], F32, name="tau_pos")
@@ -81,7 +81,8 @@ def tile_soft_thresholded_graph_laplacian_g4_kernel(tc, x, r, w_words, w_scales,
 
         xs, xt, ub, uq, us = {}, {}, {}, {}, {}
         zs, zt, yt, yb, ya, acc = {}, {}, {}, {}, {}, {}
-        y_scale = [keep.tile([P, GROUPS, 2 * BLOCK], U8, name="y_scale%d" % i, align_bytes=64) for i in range(BLOCKS // 2)]
+        scale_early = keep.tile([P, GROUPS, B - BLOCK], U8, name="scale_early", align_bytes=64)
+        scale_last = keep.tile([P, GROUPS, BLOCK], U8, name="scale_last", align_bytes=64)
 
         def sort_x(n):
             xs[n] = keep.tile([P, TILES, 2, P], F32, name="xs%d" % n)
@@ -159,7 +160,7 @@ def tile_soft_thresholded_graph_laplacian_g4_kernel(tc, x, r, w_words, w_scales,
                     )
 
         def round_y(s):
-            yb[s] = work.tile([P, BLOCK, 4], BF16, name="yb", align_bytes=64)
+            yb[s] = work.tile([P, BLOCK, 4], BF16, name="yb", align_bytes=64, bufs=1)
             src = yt[s][:].rearrange("p t m -> p m t")
             if s == STEPS - 1:
                 nc.vector.tensor_copy(out=yb[s][:], in_=src)
@@ -169,18 +170,20 @@ def tile_soft_thresholded_graph_laplacian_g4_kernel(tc, x, r, w_words, w_scales,
         def quant_y(s):
             h, g = divmod(s, GROUPS)
             codes = work.tile([P, BLOCK], U32, name="codes", align_bytes=64)
-            plane = y_scale[h // 2]
+            last = h == BLOCKS - 1
+            plane, first = (scale_last, B - BLOCK) if last else (scale_early, 0)
             nc.vector.quantize_mx(
                 out=codes[:].bitcast(FP8X4),
-                scales=plane[:, g, (h % 2) * BLOCK:(h % 2 + 1) * BLOCK],
+                scales=plane[:, g, h * BLOCK - first:(h + 1) * BLOCK - first],
                 in_=yb[s][:].rearrange("p m t -> p (m t)"),
             )
             dst = out_1[g, :, h * BLOCK:(h + 1) * BLOCK, :].rearrange("p m t -> p (m t)").bitcast(I32)
             nc.sync.dma_start(out=dst, in_=codes[:].bitcast(I32))
-            if s % (2 * GROUPS) == 2 * GROUPS - 1:
-                cols = slice((h // 2) * 2 * BLOCK, (h // 2 + 1) * 2 * BLOCK)
+            if h >= BLOCKS - 2 and g == GROUPS - 1:
+                cols = slice(first, (h + 1) * BLOCK)
+                queue = nc.scalar if last else nc.sync
                 for q in range(4):
-                    nc.sync.dma_start(
+                    queue.dma_start(
                         out=out_2[:, 4 * q:4 * q + 4, cols].bitcast(I32).rearrange("g r m -> r g m"),
                         in_=plane[32 * q:32 * q + 4, :, :].bitcast(I32),
                     )
@@ -207,42 +210,44 @@ def tile_soft_thresholded_graph_laplacian_g4_kernel(tc, x, r, w_words, w_scales,
         turn_x(1)
         scale_x(0)
         turn_x(2)
-        scale_x(1)
         quant_u(0)
-        scale_x(2)
+        scale_x(1)
         quant_u(1)
+        scale_x(2)
         quant_u(2)
         for n in range(GROUPS):
             sort_x(n)
 
         def turned_at(s):
-            if s == 0:
-                return [GROUPS, GROUPS + 1]
-            return [s + GROUPS + 1] if 0 < s < STEPS - GROUPS - 1 else []
+            if s in (0, 1):
+                return [GROUPS + 2 * s, GROUPS + 2 * s + 1]
+            return [s + GROUPS + 2] if 1 < s < STEPS - GROUPS - 2 else []
 
-        for s in range(STEPS + 2):
+        for s in range(STEPS + 1):
             if s < STEPS:
                 product(s)
             for n in turned_at(s - 1):
                 scale_x(n)
             if s < STEPS:
                 difference(s)
-            for n in turned_at(s - 1):
-                quant_u(n)
-            if 2 <= s <= STEPS:
-                quant_y(s - 2)
             for n in turned_at(s):
                 sort_x(n)
-            if 1 <= s <= STEPS:
+            if s >= 1:
                 turn_z(s - 1)
             if s >= 2:
                 turn_y(s - 2)
             for n in turned_at(s):
                 turn_x(n)
-            if 1 <= s <= STEPS:
+            if s >= 1:
                 threshold(s - 1)
-                round_y(s - 1)
-            if s == STEPS + 1:
+            for n in turned_at(s - 1):
+                quant_u(n)
+            if s >= 2:
                 quant_y(s - 2)
+            if s >= 1:
+                round_y(s - 1)
             if s >= 2:
                 store_y(s - 2)
+        turn_y(STEPS - 1)
+        store_y(STEPS - 1)
+        quant_y(STEPS - 1)

@@ -23,6 +23,7 @@ BLOCK = 256
 TILES = BLOCK // P
 BLOCKS = B // BLOCK
 STEPS = BLOCKS * GROUPS
+VECTOR_ROUNDS_FROM = 10
 
 
 def tile_soft_thresholded_graph_laplacian_g4_kernel(tc, x, r, w_words, w_scales, tau, out_0, out_1, out_2):
@@ -33,10 +34,12 @@ def tile_soft_thresholded_graph_laplacian_g4_kernel(tc, x, r, w_words, w_scales,
         psum = ctx.enter_context(tc.psum_pool(name="psum", bufs=2))
         ctx.enter_context(tc.manual_schedule())
 
+        scale_first = keep.tile([P, GROUPS, GROUP], U8, name="scale_first", align_bytes=64)
+        scale_rest = keep.tile([P, GROUPS, N - GROUP], U8, name="scale_rest", align_bytes=64)
+        nc.vector.memset(scale_first[:].rearrange("p g n -> p (g n)").bitcast(I32), 0)
         ident = keep.tile([P, P], F32, name="ident")
         make_identity(nc, ident[:])
-        w_scale = keep.tile([P, GROUPS, N], U8, name="w_scale", align_bytes=64)
-        nc.vector.memset(w_scale[:].rearrange("p g n -> p (g n)").bitcast(I32), 0)
+        nc.vector.memset(scale_rest[:].rearrange("p g n -> p (g n)").bitcast(I32), 0)
 
         raw = {}
 
@@ -49,47 +52,54 @@ def tile_soft_thresholded_graph_laplacian_g4_kernel(tc, x, r, w_words, w_scales,
 
         w_code = {}
 
-        def load_w(g):
-            t = keep.tile([P, GROUPS, 2 * GROUP], U8, name="w_code%d" % g, align_bytes=64)
-            src = w_words[:, :, 2 * GROUP * g:2 * GROUP * (g + 1)].bitcast(I32).rearrange("k p n -> p k n")
+        def load_w(g, k0, k1):
+            t = keep.tile([P, k1 - k0, 2 * GROUP], U8, name="w_code%d_%d" % (g, k0), align_bytes=64)
+            src = w_words[k0:k1, :, 2 * GROUP * g:2 * GROUP * (g + 1)].bitcast(I32).rearrange("k p n -> p k n")
             nc.sync.dma_start(out=t[:].bitcast(I32), in_=src)
-            w_code[g] = t
+            for k in range(k0, k1):
+                w_code[g, k] = t[:, k - k0, :]
+
+        def load_w_scales(queue, plane, q, cols):
+            queue.dma_start(
+                out=plane[32 * q:32 * q + 4, :, :].bitcast(I32),
+                in_=w_scales[:, 4 * q:4 * q + 4, cols].bitcast(I32).rearrange("k r n -> r k n"),
+            )
 
         r_sb = keep.tile([P, GROUPS, 4], BF16, name="r_sb")
         tau_sb = keep.tile([P, GROUPS, 4], BF16, name="tau_sb")
         load_x(0, 0, 1, "x_first")
         nc.scalar.dma_start(out=r_sb[:], in_=r.rearrange("(g p t) -> p g t", p=P, t=4))
         load_x(0, 1, GROUPS, "x_rest")
-        load_w(0)
+        load_w(0, 0, 1)
         for q in range(4):
-            nc.scalar.dma_start(
-                out=w_scale[32 * q:32 * q + 4, :, :].bitcast(I32),
-                in_=w_scales[:, 4 * q:4 * q + 4, :].bitcast(I32).rearrange("k r n -> r k n"),
-            )
-        nc.sync.dma_start(out=tau_sb[:], in_=tau.rearrange("(g p t) -> p g t", p=P, t=4))
+            load_w_scales(nc.scalar if q < 2 else nc.sync, scale_first, q, slice(0, GROUP))
+        load_w(0, 1, GROUPS)
         load_x(1, 0, GROUPS, "x_1")
-        load_w(1)
+        nc.gpsimd.dma_start(out=tau_sb[:], in_=tau.rearrange("(g p t) -> p g t", p=P, t=4))
+        for q in range(4):
+            load_w_scales(nc.gpsimd, scale_rest, q, slice(GROUP, N))
+        for g in range(1, GROUPS):
+            load_w(g, 0, 1)
+            load_w(g, 1, GROUPS)
         load_x(2, 0, GROUPS, "x_2")
-        load_w(2)
         load_x(3, 0, GROUPS, "x_3")
 
         tau_pos = keep.tile([P, GROUPS * 4], F32, name="tau_pos")
         tau_neg = keep.tile([P, GROUPS * 4], F32, name="tau_neg")
         tau_flat = tau_sb[:].rearrange("p g t -> p (g t)")
-        nc.gpsimd.tensor_scalar(tau_pos[:], tau_flat, 1.0, 0.0, ALU.mult, ALU.add)
-        nc.scalar.activation(out=tau_neg[:], in_=tau_flat, func=ACT.Copy, scale=-1.0)
 
         xs, xt, ub, uq, us = {}, {}, {}, {}, {}
         zs, zt, yt, yb, ya, acc = {}, {}, {}, {}, {}, {}
-        scale_early = keep.tile([P, GROUPS, B - BLOCK], U8, name="scale_early", align_bytes=64)
-        scale_last = keep.tile([P, GROUPS, BLOCK], U8, name="scale_last", align_bytes=64)
+        y_scale_first = keep.tile([P, 1, B], U8, name="y_scale_first", align_bytes=64)
+        y_scale_rest = keep.tile([P, GROUPS - 1, B], U8, name="y_scale_rest", align_bytes=64)
+        codes_last = keep.tile([P, 2, BLOCK], U32, name="codes_last", align_bytes=64)
 
         def sort_x(n):
             xs[n] = keep.tile([P, TILES, 2, P], F32, name="xs%d" % n)
             nc.scalar.copy(out=xs[n][:], in_=raw[n].bitcast(F32).rearrange("b i (p u) -> b i u p", u=2))
 
         def turn_x(n):
-            xt[n] = psum.tile([P, 2, TILES, P], F32, name="xt")
+            xt[n] = psum.tile([P, 2, TILES, P], F32, name="zt" if n == 2 * GROUPS - 1 else "xt")
             for i in range(TILES):
                 for u in range(2):
                     if n < GROUPS:
@@ -99,7 +109,7 @@ def tile_soft_thresholded_graph_laplacian_g4_kernel(tc, x, r, w_words, w_scales,
                     nc.tensor.transpose(xt[n][:, u, i, :], src, ident[:])
 
         def scale_x(n):
-            ub[n] = work.tile([P, BLOCK, 2, 2], BF16, name="ub", align_bytes=64)
+            ub[n] = work.tile([P, BLOCK, 2, 2], BF16, name="ub", align_bytes=64, bufs=4)
             src = xt[n][:].rearrange("p u i b -> p (u i b)").bitcast(BF16).rearrange("p (u m e) -> p m u e", u=2, e=2)
             fac = r_sb[:, n % GROUPS, :].rearrange("p (u e) -> p u e", u=2).unsqueeze(1).to_broadcast([P, BLOCK, 2, 2])
             nc.vector.tensor_tensor(out=ub[n][:], in0=src, in1=fac, op=ALU.mult)
@@ -121,8 +131,8 @@ def tile_soft_thresholded_graph_laplacian_g4_kernel(tc, x, r, w_words, w_scales,
                     out=acc[s][i][:],
                     lhsT=uq[n][:, i * P:(i + 1) * P].bitcast(FP8X4),
                     lhsT_scale=us[n][:, i * P:(i + 1) * P],
-                    rhs=w_code[g][:, k, :].bitcast(FP4X4),
-                    rhs_scale=w_scale[:, k, g * GROUP:(g + 1) * GROUP],
+                    rhs=w_code[g, k].bitcast(FP4X4),
+                    rhs_scale=scale_first[:, k, :] if g == 0 else scale_rest[:, k, (g - 1) * GROUP:g * GROUP],
                     start=(k == 0),
                     stop=(k == GROUPS - 1),
                 )
@@ -137,7 +147,7 @@ def tile_soft_thresholded_graph_laplacian_g4_kernel(tc, x, r, w_words, w_scales,
                 zs[s].append(z)
 
         def turn_z(s):
-            zt[s] = [psum.tile([P, 2, TILES, P], F32, name="zt") for u in range(2)]
+            zt[s] = [psum.tile([P, 2, TILES, P], F32, name="xt" if s == STEPS - 2 else "zt") for u in range(2)]
             for u in range(2):
                 for e in range(2):
                     for i in range(TILES):
@@ -160,33 +170,40 @@ def tile_soft_thresholded_graph_laplacian_g4_kernel(tc, x, r, w_words, w_scales,
                     )
 
         def round_y(s):
-            yb[s] = work.tile([P, BLOCK, 4], BF16, name="yb", align_bytes=64, bufs=1)
             src = yt[s][:].rearrange("p t m -> p m t")
-            if s == STEPS - 1:
+            if s >= VECTOR_ROUNDS_FROM:
+                yb[s] = work.tile([P, BLOCK, 4], BF16, name="yb_late", align_bytes=64, bufs=2)
                 nc.vector.tensor_copy(out=yb[s][:], in_=src)
             else:
+                yb[s] = work.tile([P, BLOCK, 4], BF16, name="yb", align_bytes=64, bufs=1)
                 nc.gpsimd.tensor_scalar(yb[s][:], src, 1.0, -0.0, ALU.mult, ALU.add)
 
         def quant_y(s):
             h, g = divmod(s, GROUPS)
-            codes = work.tile([P, BLOCK], U32, name="codes", align_bytes=64)
-            last = h == BLOCKS - 1
-            plane, first = (scale_last, B - BLOCK) if last else (scale_early, 0)
-            nc.vector.quantize_mx(
-                out=codes[:].bitcast(FP8X4),
-                scales=plane[:, g, h * BLOCK - first:(h + 1) * BLOCK - first],
-                in_=yb[s][:].rearrange("p m t -> p (m t)"),
-            )
-            dst = out_1[g, :, h * BLOCK:(h + 1) * BLOCK, :].rearrange("p m t -> p (m t)").bitcast(I32)
-            nc.sync.dma_start(out=dst, in_=codes[:].bitcast(I32))
-            if h >= BLOCKS - 2 and g == GROUPS - 1:
-                cols = slice(first, (h + 1) * BLOCK)
-                queue = nc.scalar if last else nc.sync
-                for q in range(4):
-                    queue.dma_start(
-                        out=out_2[:, 4 * q:4 * q + 4, cols].bitcast(I32).rearrange("g r m -> r g m"),
-                        in_=plane[32 * q:32 * q + 4, :, :].bitcast(I32),
-                    )
+            cols = slice(h * BLOCK, (h + 1) * BLOCK)
+            plane = y_scale_first[:, 0, cols] if g == 0 else y_scale_rest[:, g - 1, cols]
+            if s < STEPS - 2:
+                codes_tile = work.tile([P, BLOCK], U32, name="codes", align_bytes=64)
+                codes = codes_tile[:]
+            else:
+                codes = codes_last[:, g - 1, :]
+            nc.vector.quantize_mx(out=codes.bitcast(FP8X4), scales=plane, in_=yb[s][:].rearrange("p m t -> p (m t)"))
+            if s < STEPS - 2:
+                dst = out_1[g, :, cols, :].rearrange("p m t -> p (m t)").bitcast(I32)
+                nc.sync.dma_start(out=dst, in_=codes.bitcast(I32))
+            if s == STEPS - 1:
+                dst = out_1[1:GROUPS, :, cols, :].rearrange("g p m t -> p g (m t)").bitcast(I32)
+                nc.sync.dma_start(out=dst, in_=codes_last[:].bitcast(I32))
+                store_scales(nc.scalar, y_scale_rest, 1, GROUPS)
+            if s == STEPS - GROUPS:
+                store_scales(nc.sync, y_scale_first, 0, 1)
+
+        def store_scales(queue, plane, g0, g1):
+            for q in range(4):
+                queue.dma_start(
+                    out=out_2[g0:g1, 4 * q:4 * q + 4, :].bitcast(I32).rearrange("g r m -> r g m"),
+                    in_=plane[32 * q:32 * q + 4, :, :].bitcast(I32),
+                )
 
         def turn_y(s):
             ya[s] = [psum.tile([P, 4, P], F32, name="ya") for i in range(TILES)]
@@ -196,13 +213,18 @@ def tile_soft_thresholded_graph_laplacian_g4_kernel(tc, x, r, w_words, w_scales,
 
         def store_y(s):
             h, g = divmod(s, GROUPS)
+            dst = out_0[h * BLOCK:(h + 1) * BLOCK, g * GROUP:(g + 1) * GROUP].rearrange("(i b) n -> b i n", b=P)
+            rows = work.tile([P, TILES, P, 4], F32, name="rows")
             for i in range(TILES):
-                rows = work.tile([P, P, 4], F32, name="rows", bufs=4)
-                src = ya[s][i][:].rearrange("b t p -> b p t")
-                if s == STEPS - 1 and i == TILES - 1:
-                    nc.vector.tensor_copy(out=rows[:], in_=src)
-                else:
-                    nc.scalar.copy(out=rows[:], in_=src)
+                nc.scalar.copy(out=rows[:, i, :, :], in_=ya[s][i][:].rearrange("b t p -> b p t"))
+            nc.sync.dma_start(out=dst, in_=rows[:].rearrange("b i p t -> b i (p t)"))
+
+        def store_last(s):
+            h, g = divmod(s, GROUPS)
+            for i in range(TILES):
+                rows = keep.tile([P, P, 4], F32, name="rows_last%d" % i)
+                copy = nc.scalar.copy if i == 0 else nc.vector.tensor_copy
+                copy(out=rows[:], in_=ya[s][i][:].rearrange("b t p -> b p t"))
                 b0 = h * BLOCK + i * P
                 nc.sync.dma_start(out=out_0[b0:b0 + P, g * GROUP:(g + 1) * GROUP], in_=rows[:].rearrange("b p t -> b (p t)"))
 
@@ -217,11 +239,13 @@ def tile_soft_thresholded_graph_laplacian_g4_kernel(tc, x, r, w_words, w_scales,
         quant_u(2)
         for n in range(GROUPS):
             sort_x(n)
+        nc.scalar.activation(out=tau_neg[:], in_=tau_flat, func=ACT.Copy, scale=-1.0)
+        nc.scalar.copy(out=tau_pos[:], in_=tau_flat)
 
         def turned_at(s):
-            if s in (0, 1):
-                return [GROUPS + 2 * s, GROUPS + 2 * s + 1]
-            return [s + GROUPS + 2] if 1 < s < STEPS - GROUPS - 2 else []
+            if s == 0:
+                return list(range(GROUPS, 2 * GROUPS))
+            return [s + GROUPS + 2] if 0 < s < STEPS - GROUPS - 2 else []
 
         for s in range(STEPS + 1):
             if s < STEPS:
@@ -238,10 +262,14 @@ def tile_soft_thresholded_graph_laplacian_g4_kernel(tc, x, r, w_words, w_scales,
                 turn_y(s - 2)
             for n in turned_at(s):
                 turn_x(n)
+            if s == 1:
+                for n in turned_at(s - 1):
+                    quant_u(n)
             if s >= 1:
                 threshold(s - 1)
-            for n in turned_at(s - 1):
-                quant_u(n)
+            if s != 1:
+                for n in turned_at(s - 1):
+                    quant_u(n)
             if s >= 2:
                 quant_y(s - 2)
             if s >= 1:
@@ -249,5 +277,5 @@ def tile_soft_thresholded_graph_laplacian_g4_kernel(tc, x, r, w_words, w_scales,
             if s >= 2:
                 store_y(s - 2)
         turn_y(STEPS - 1)
-        store_y(STEPS - 1)
+        store_last(STEPS - 1)
         quant_y(STEPS - 1)

@@ -34,17 +34,17 @@ def tile_soft_thresholded_graph_laplacian_g4_kernel(tc, x, r, w_words, w_scales,
         psum = ctx.enter_context(tc.psum_pool(name="psum", bufs=2))
         ctx.enter_context(tc.manual_schedule())
 
-        scale_first = keep.tile([P, GROUPS, GROUP], U8, name="scale_first", align_bytes=64)
-        scale_rest = keep.tile([P, GROUPS, N - GROUP], U8, name="scale_rest", align_bytes=64)
+        scale_first = keep.tile([P, GROUPS, GROUP], U8, name="scale_first", align_bytes=256)
+        scale_rest = keep.tile([P, GROUPS, N - GROUP], U8, name="scale_rest", align_bytes=256)
         nc.vector.memset(scale_first[:].rearrange("p g n -> p (g n)").bitcast(I32), 0)
-        ident = keep.tile([P, P], F32, name="ident")
+        ident = keep.tile([P, P], F32, name="ident", align_bytes=256)
         make_identity(nc, ident[:])
         nc.vector.memset(scale_rest[:].rearrange("p g n -> p (g n)").bitcast(I32), 0)
 
         raw = {}
 
         def load_x(h, k0, k1, name):
-            t = keep.tile([P, TILES, (k1 - k0) * GROUP], BF16, name=name)
+            t = keep.tile([P, TILES, (k1 - k0) * GROUP], BF16, name=name, align_bytes=256)
             src = x[h * BLOCK:(h + 1) * BLOCK, k0 * GROUP:k1 * GROUP].rearrange("(i p) n -> p i n", p=P)
             nc.sync.dma_start(out=t[:], in_=src)
             for k in range(k0, k1):
@@ -53,7 +53,7 @@ def tile_soft_thresholded_graph_laplacian_g4_kernel(tc, x, r, w_words, w_scales,
         w_code = {}
 
         def load_w(g, k0, k1):
-            t = keep.tile([P, k1 - k0, 2 * GROUP], U8, name="w_code%d_%d" % (g, k0), align_bytes=64)
+            t = keep.tile([P, k1 - k0, 2 * GROUP], U8, name="w_code%d_%d" % (g, k0), align_bytes=256)
             src = w_words[k0:k1, :, 2 * GROUP * g:2 * GROUP * (g + 1)].bitcast(I32).rearrange("k p n -> p k n")
             nc.sync.dma_start(out=t[:].bitcast(I32), in_=src)
             for k in range(k0, k1):
@@ -90,12 +90,12 @@ def tile_soft_thresholded_graph_laplacian_g4_kernel(tc, x, r, w_words, w_scales,
 
         xs, xt, ub, uq, us = {}, {}, {}, {}, {}
         zs, zt, yt, yb, ya, acc = {}, {}, {}, {}, {}, {}
-        y_scale_first = keep.tile([P, 1, B], U8, name="y_scale_first", align_bytes=64)
-        y_scale_rest = keep.tile([P, GROUPS - 1, B], U8, name="y_scale_rest", align_bytes=64)
-        codes_last = keep.tile([P, 2, BLOCK], U32, name="codes_last", align_bytes=64)
+        y_scale_first = keep.tile([P, 1, B], U8, name="y_scale_first", align_bytes=256)
+        y_scale_rest = keep.tile([P, GROUPS - 1, B], U8, name="y_scale_rest", align_bytes=256)
+        codes_last = keep.tile([P, 2, BLOCK], U32, name="codes_last", align_bytes=256)
 
         def sort_x(n):
-            xs[n] = keep.tile([P, TILES, 2, P], F32, name="xs%d" % n)
+            xs[n] = keep.tile([P, TILES, 2, P], F32, name="xs%d" % n, align_bytes=256)
             nc.scalar.copy(out=xs[n][:], in_=raw[n].bitcast(F32).rearrange("b i (p u) -> b i u p", u=2))
 
         def turn_x(n):
@@ -109,14 +109,14 @@ def tile_soft_thresholded_graph_laplacian_g4_kernel(tc, x, r, w_words, w_scales,
                     nc.tensor.transpose(xt[n][:, u, i, :], src, ident[:])
 
         def scale_x(n):
-            ub[n] = work.tile([P, BLOCK, 2, 2], BF16, name="ub", align_bytes=64, bufs=4)
+            ub[n] = work.tile([P, BLOCK, 2, 2], BF16, name="ub", align_bytes=256, bufs=4)
             src = xt[n][:].rearrange("p u i b -> p (u i b)").bitcast(BF16).rearrange("p (u m e) -> p m u e", u=2, e=2)
             fac = r_sb[:, n % GROUPS, :].rearrange("p (u e) -> p u e", u=2).unsqueeze(1).to_broadcast([P, BLOCK, 2, 2])
             nc.vector.tensor_tensor(out=ub[n][:], in0=src, in1=fac, op=ALU.mult)
 
         def quant_u(n):
-            uq[n] = keep.tile([P, BLOCK], U32, name="uq%d" % n, align_bytes=64)
-            us[n] = keep.tile([P, BLOCK], U8, name="us%d" % n, align_bytes=64)
+            uq[n] = keep.tile([P, BLOCK], U32, name="uq%d" % n, align_bytes=256)
+            us[n] = keep.tile([P, BLOCK], U8, name="us%d" % n, align_bytes=256)
             nc.vector.quantize_mx(out=uq[n][:].bitcast(FP8X4), scales=us[n][:], in_=ub[n][:].rearrange("p m u e -> p (m u e)"))
 
         def product(s):
@@ -140,7 +140,7 @@ def tile_soft_thresholded_graph_laplacian_g4_kernel(tc, x, r, w_words, w_scales,
         def difference(s):
             zs[s] = []
             for i in range(TILES):
-                z = work.tile([P, 2, 2, P], F32, name="zs", bufs=2 * TILES + 1)
+                z = work.tile([P, 2, 2, P], F32, name="zs", align_bytes=256, bufs=2 * TILES + 1)
                 xv = xs[s][:, i, :, :].rearrange("b u p -> b (u p)").bitcast(BF16).rearrange("b (u p e) -> b u e p", u=2, e=2)
                 av = acc[s][i][:].rearrange("b (p u e) -> b u e p", u=2, e=2)
                 nc.vector.tensor_tensor(out=z[:], in0=xv, in1=av, op=ALU.subtract)
@@ -155,9 +155,9 @@ def tile_soft_thresholded_graph_laplacian_g4_kernel(tc, x, r, w_words, w_scales,
 
         def threshold(s):
             g = s % GROUPS
-            yt[s] = work.tile([P, 4, BLOCK], F32, name="yt")
+            yt[s] = work.tile([P, 4, BLOCK], F32, name="yt", align_bytes=256)
             for u in range(2):
-                above = work.tile([P, 2, BLOCK], F32, name="above")
+                above = work.tile([P, 2, BLOCK], F32, name="above", align_bytes=256)
                 for e in range(2):
                     c = 4 * g + 2 * u + e
                     zv = zt[s][u][:, e, :, :].rearrange("p i b -> p (i b)")
@@ -172,10 +172,10 @@ def tile_soft_thresholded_graph_laplacian_g4_kernel(tc, x, r, w_words, w_scales,
         def round_y(s):
             src = yt[s][:].rearrange("p t m -> p m t")
             if s >= VECTOR_ROUNDS_FROM:
-                yb[s] = work.tile([P, BLOCK, 4], BF16, name="yb_late", align_bytes=64, bufs=2)
+                yb[s] = work.tile([P, BLOCK, 4], BF16, name="yb_late", align_bytes=256, bufs=2)
                 nc.vector.tensor_copy(out=yb[s][:], in_=src)
             else:
-                yb[s] = work.tile([P, BLOCK, 4], BF16, name="yb", align_bytes=64, bufs=1)
+                yb[s] = work.tile([P, BLOCK, 4], BF16, name="yb", align_bytes=256, bufs=1)
                 nc.gpsimd.tensor_scalar(yb[s][:], src, 1.0, -0.0, ALU.mult, ALU.add)
 
         def quant_y(s):
@@ -183,7 +183,7 @@ def tile_soft_thresholded_graph_laplacian_g4_kernel(tc, x, r, w_words, w_scales,
             cols = slice(h * BLOCK, (h + 1) * BLOCK)
             plane = y_scale_first[:, 0, cols] if g == 0 else y_scale_rest[:, g - 1, cols]
             if s < STEPS - 2:
-                codes_tile = work.tile([P, BLOCK], U32, name="codes", align_bytes=64)
+                codes_tile = work.tile([P, BLOCK], U32, name="codes", align_bytes=256)
                 codes = codes_tile[:]
             else:
                 codes = codes_last[:, g - 1, :]
@@ -214,7 +214,7 @@ def tile_soft_thresholded_graph_laplacian_g4_kernel(tc, x, r, w_words, w_scales,
         def store_y(s):
             h, g = divmod(s, GROUPS)
             dst = out_0[h * BLOCK:(h + 1) * BLOCK, g * GROUP:(g + 1) * GROUP].rearrange("(i b) n -> b i n", b=P)
-            rows = work.tile([P, TILES, P, 4], F32, name="rows")
+            rows = work.tile([P, TILES, P, 4], F32, name="rows", align_bytes=256)
             for i in range(TILES):
                 nc.scalar.copy(out=rows[:, i, :, :], in_=ya[s][i][:].rearrange("b t p -> b p t"))
             nc.sync.dma_start(out=dst, in_=rows[:].rearrange("b i p t -> b i (p t)"))
@@ -226,7 +226,8 @@ def tile_soft_thresholded_graph_laplacian_g4_kernel(tc, x, r, w_words, w_scales,
                 copy = nc.scalar.copy if i == 0 else nc.vector.tensor_copy
                 copy(out=rows[:], in_=ya[s][i][:].rearrange("b t p -> b p t"))
                 b0 = h * BLOCK + i * P
-                nc.sync.dma_start(out=out_0[b0:b0 + P, g * GROUP:(g + 1) * GROUP], in_=rows[:].rearrange("b p t -> b (p t)"))
+                queue = nc.scalar if i == 0 else nc.sync
+                queue.dma_start(out=out_0[b0:b0 + P, g * GROUP:(g + 1) * GROUP], in_=rows[:].rearrange("b p t -> b (p t)"))
 
         turn_x(0)
         turn_x(1)

@@ -76,12 +76,13 @@ def tile_soft_thresholded_graph_laplacian_g4_kernel(tc, x, r, w_words, w_scales,
         load_w(0, 1, GROUPS)
         load_x(1, 0, GROUPS, "x_1")
         nc.gpsimd.dma_start(out=tau_sb[:], in_=tau.rearrange("(g p t) -> p g t", p=P, t=4))
+        load_w(1, 0, 1)
+        load_w(1, 1, GROUPS)
         for q in range(4):
-            load_w_scales(nc.gpsimd, scale_rest, q, slice(GROUP, N))
-        for g in range(1, GROUPS):
-            load_w(g, 0, 1)
-            load_w(g, 1, GROUPS)
+            load_w_scales(nc.sync, scale_rest, q, slice(GROUP, N))
         load_x(2, 0, GROUPS, "x_2")
+        load_w(2, 0, 1)
+        load_w(2, 1, GROUPS)
         load_x(3, 0, GROUPS, "x_3")
 
         tau_pos = keep.tile([P, GROUPS * 4], F32, name="tau_pos")
@@ -240,8 +241,6 @@ def tile_soft_thresholded_graph_laplacian_g4_kernel(tc, x, r, w_words, w_scales,
         quant_u(2)
         for n in range(GROUPS):
             sort_x(n)
-        nc.scalar.activation(out=tau_neg[:], in_=tau_flat, func=ACT.Copy, scale=-1.0)
-        nc.scalar.copy(out=tau_pos[:], in_=tau_flat)
 
         def turned_at(s):
             if s == 0:
@@ -257,6 +256,9 @@ def tile_soft_thresholded_graph_laplacian_g4_kernel(tc, x, r, w_words, w_scales,
                 difference(s)
             for n in turned_at(s):
                 sort_x(n)
+            if s == 0:
+                nc.scalar.activation(out=tau_neg[:], in_=tau_flat, func=ACT.Copy, scale=-1.0)
+                nc.scalar.copy(out=tau_pos[:], in_=tau_flat)
             if s >= 1:
                 turn_z(s - 1)
             if s >= 2:

from contextlib import ExitStack

import concourse.mybir as mybir
from concourse.masks import make_identity

B, N = 1024, 1536
FLOPS = 2 * B * N * N

F32 = mybir.dt.float32
BF16 = mybir.dt.bfloat16
I32 = mybir.dt.int32
U32 = mybir.dt.uint32
U8 = mybir.dt.uint8
FP8X4 = mybir.dt.float8_e4m3fn_x4
FP4X4 = mybir.dt.float4_e2m1fn_x4
ALU = mybir.AluOpType
ACT = mybir.ActivationFunctionType

P = 128
GROUP = 512
GROUPS = N // GROUP
BLOCK = 256
TILES = BLOCK // P
BLOCKS = B // BLOCK
STEPS = BLOCKS * GROUPS
VECTOR_ROUNDS_FROM = 10


def tile_soft_thresholded_graph_laplacian_g4_kernel(tc, x, r, w_words, w_scales, tau, out_0, out_1, out_2):
    nc = tc.nc
    with ExitStack() as ctx:
        keep = ctx.enter_context(tc.tile_pool(name="keep", bufs=1))
        work = ctx.enter_context(tc.tile_pool(name="work", bufs=3))
        psum = ctx.enter_context(tc.psum_pool(name="psum", bufs=2))
        ctx.enter_context(tc.manual_schedule())

        scale_first = keep.tile([P, GROUPS, GROUP], U8, name="scale_first", align_bytes=256)
        scale_rest = keep.tile([P, GROUPS, N - GROUP], U8, name="scale_rest", align_bytes=256)
        nc.vector.memset(scale_first[:].rearrange("p g n -> p (g n)").bitcast(I32), 0)
        ident = keep.tile([P, P], F32, name="ident", align_bytes=256)
        make_identity(nc, ident[:])
        nc.vector.memset(scale_rest[:].rearrange("p g n -> p (g n)").bitcast(I32), 0)

        raw = {}

        def load_x(h, k0, k1, name):
            t = keep.tile([P, TILES, (k1 - k0) * GROUP], BF16, name=name, align_bytes=256)
            src = x[h * BLOCK:(h + 1) * BLOCK, k0 * GROUP:k1 * GROUP].rearrange("(i p) n -> p i n", p=P)
            nc.sync.dma_start(out=t[:], in_=src)
            for k in range(k0, k1):
                raw[h * GROUPS + k] = t[:, :, (k - k0) * GROUP:(k - k0 + 1) * GROUP]

        w_code = {}

        def load_w(g, k0, k1):
            t = keep.tile([P, k1 - k0, 2 * GROUP], U8, name="w_code%d_%d" % (g, k0), align_bytes=256)
            src = w_words[k0:k1, :, 2 * GROUP * g:2 * GROUP * (g + 1)].bitcast(I32).rearrange("k p n -> p k n")
            nc.sync.dma_start(out=t[:].bitcast(I32), in_=src)
            for k in range(k0, k1):
                w_code[g, k] = t[:, k - k0, :]

        def load_w_scales(queue, plane, q, cols):
            queue.dma_start(
                out=plane[32 * q:32 * q + 4, :, :].bitcast(I32),
                in_=w_scales[:, 4 * q:4 * q + 4, cols].bitcast(I32).rearrange("k r n -> r k n"),
            )

        r_sb = keep.tile([P, GROUPS, 4], BF16, name="r_sb")
        tau_sb = keep.tile([P, GROUPS, 4], BF16, name="tau_sb")
        load_x(0, 0, 1, "x_first")
        nc.scalar.dma_start(out=r_sb[:], in_=r.rearrange("(g p t) -> p g t", p=P, t=4))
        load_x(0, 1, GROUPS, "x_rest")
        load_w(0, 0, 1)
        for q in range(4):
            load_w_scales(nc.scalar if q < 2 else nc.sync, scale_first, q, slice(0, GROUP))
        load_w(0, 1, GROUPS)
        load_x(1, 0, GROUPS, "x_1")
        nc.gpsimd.dma_start(out=tau_sb[:], in_=tau.rearrange("(g p t) -> p g t", p=P, t=4))
        load_w(1, 0, 1)
        load_w(1, 1, GROUPS)
        for q in range(4):
            load_w_scales(nc.sync, scale_rest, q, slice(GROUP, N))
        load_x(2, 0, GROUPS, "x_2")
        load_w(2, 0, 1)
        load_w(2, 1, GROUPS)
        load_x(3, 0, GROUPS, "x_3")

        tau_pos = keep.tile([P, GROUPS * 4], F32, name="tau_pos")
        tau_neg = keep.tile([P, GROUPS * 4], F32, name="tau_neg")
        tau_flat = tau_sb[:].rearrange("p g t -> p (g t)")

        xs, xt, ub, uq, us = {}, {}, {}, {}, {}
        zs, zt, yt, yb, ya, acc = {}, {}, {}, {}, {}, {}
        y_scale_first = keep.tile([P, 1, B], U8, name="y_scale_first", align_bytes=256)
        y_scale_rest = keep.tile([P, GROUPS - 1, B], U8, name="y_scale_rest", align_bytes=256)
        codes_last = keep.tile([P, 2, BLOCK], U32, name="codes_last", align_bytes=256)

        def sort_x(n):
            xs[n] = keep.tile([P, TILES, 2, P], F32, name="xs%d" % n, align_bytes=256)
            nc.scalar.copy(out=xs[n][:], in_=raw[n].bitcast(F32).rearrange("b i (p u) -> b i u p", u=2))

        def turn_x(n):
            xt[n] = psum.tile([P, 2, TILES, P], F32, name="zt" if n == 2 * GROUPS - 1 else "xt")
            for i in range(TILES):
                for u in range(2):
                    if n < GROUPS:
                        src = raw[n].bitcast(F32)[:, i, u::2]
                    else:
                        src = xs[n][:, i, u, :]
                    nc.tensor.transpose(xt[n][:, u, i, :], src, ident[:])

        def scale_x(n):
            ub[n] = work.tile([P, BLOCK, 2, 2], BF16, name="ub", align_bytes=256, bufs=4)
            src = xt[n][:].rearrange("p u i b -> p (u i b)").bitcast(BF16).rearrange("p (u m e) -> p m u e", u=2, e=2)
            fac = r_sb[:, n % GROUPS, :].rearrange("p (u e) -> p u e", u=2).unsqueeze(1).to_broadcast([P, BLOCK, 2, 2])
            nc.vector.tensor_tensor(out=ub[n][:], in0=src, in1=fac, op=ALU.mult)

        def quant_u(n):
            uq[n] = keep.tile([P, BLOCK], U32, name="uq%d" % n, align_bytes=256)
            us[n] = keep.tile([P, BLOCK], U8, name="us%d" % n, align_bytes=256)
            nc.vector.quantize_mx(out=uq[n][:].bitcast(FP8X4), scales=us[n][:], in_=ub[n][:].rearrange("p m u e -> p (m u e)"))

        def product(s):
            h, g = divmod(s, GROUPS)
            acc[s] = [psum.tile([P, GROUP], F32, name="acc") for i in range(TILES)]
            order = [(i, k) for i in range(TILES) for k in range(GROUPS)]
            if s == 0:
                order = [(i, k) for k in range(GROUPS) for i in range(TILES)]
            for i, k in order:
                n = h * GROUPS + k
                nc.tensor.matmul_mx(
                    out=acc[s][i][:],
                    lhsT=uq[n][:, i * P:(i + 1) * P].bitcast(FP8X4),
                    lhsT_scale=us[n][:, i * P:(i + 1) * P],
                    rhs=w_code[g, k].bitcast(FP4X4),
                    rhs_scale=scale_first[:, k, :] if g == 0 else scale_rest[:, k, (g - 1) * GROUP:g * GROUP],
                    start=(k == 0),
                    stop=(k == GROUPS - 1),
                )

        def difference(s):
            zs[s] = []
            for i in range(TILES):
                z = work.tile([P, 2, 2, P], F32, name="zs", align_bytes=256, bufs=2 * TILES + 1)
                xv = xs[s][:, i, :, :].rearrange("b u p -> b (u p)").bitcast(BF16).rearrange("b (u p e) -> b u e p", u=2, e=2)
                av = acc[s][i][:].rearrange("b (p u e) -> b u e p", u=2, e=2)
                nc.vector.tensor_tensor(out=z[:], in0=xv, in1=av, op=ALU.subtract)
                zs[s].append(z)

        def turn_z(s):
            zt[s] = [psum.tile([P, 2, TILES, P], F32, name="xt" if s == STEPS - 2 else "zt") for u in range(2)]
            for u in range(2):
                for e in range(2):
                    for i in range(TILES):
                        nc.tensor.transpose(zt[s][u][:, e, i, :], zs[s][i][:, u, e, :], ident[:])

        def threshold(s):
            g = s % GROUPS
            yt[s] = work.tile([P, 4, BLOCK], F32, name="yt", align_bytes=256)
            for u in range(2):
                above = work.tile([P, 2, BLOCK], F32, name="above", align_bytes=256)
                for e in range(2):
                    c = 4 * g + 2 * u + e
                    zv = zt[s][u][:, e, :, :].rearrange("p i b -> p (i b)")
                    nc.scalar.activation(out=above[:, e, :], in_=zv, func=ACT.Relu, bias=tau_neg[:, c:c + 1])
                for e in range(2):
                    c = 4 * g + 2 * u + e
                    zv = zt[s][u][:, e, :, :].rearrange("p i b -> p (i b)")
                    nc.vector.scalar_tensor_tensor(
                        out=yt[s][:, 2 * u + e, :], in0=zv, scalar=tau_pos[:, c:c + 1], in1=above[:, e, :], op0=ALU.add, op1=ALU.min
                    )

        def round_y(s):
            src = yt[s][:].rearrange("p t m -> p m t")
            if s >= VECTOR_ROUNDS_FROM:
                yb[s] = work.tile([P, BLOCK, 4], BF16, name="yb_late", align_bytes=256, bufs=2)
                nc.vector.tensor_copy(out=yb[s][:], in_=src)
            else:
                yb[s] = work.tile([P, BLOCK, 4], BF16, name="yb", align_bytes=256, bufs=1)
                nc.gpsimd.tensor_scalar(yb[s][:], src, 1.0, -0.0, ALU.mult, ALU.add)

        def quant_y(s):
            h, g = divmod(s, GROUPS)
            cols = slice(h * BLOCK, (h + 1) * BLOCK)
            plane = y_scale_first[:, 0, cols] if g == 0 else y_scale_rest[:, g - 1, cols]
            if s < STEPS - 2:
                codes_tile = work.tile([P, BLOCK], U32, name="codes", align_bytes=256)
                codes = codes_tile[:]
            else:
                codes = codes_last[:, g - 1, :]
            nc.vector.quantize_mx(out=codes.bitcast(FP8X4), scales=plane, in_=yb[s][:].rearrange("p m t -> p (m t)"))
            if s < STEPS - 2:
                dst = out_1[g, :, cols, :].rearrange("p m t -> p (m t)").bitcast(I32)
                nc.sync.dma_start(out=dst, in_=codes.bitcast(I32))
            if s == STEPS - 1:
                dst = out_1[1:GROUPS, :, cols, :].rearrange("g p m t -> p g (m t)").bitcast(I32)
                nc.sync.dma_start(out=dst, in_=codes_last[:].bitcast(I32))
                store_scales(nc.scalar, y_scale_rest, 1, GROUPS)
            if s == STEPS - GROUPS:
                store_scales(nc.sync, y_scale_first, 0, 1)

        def store_scales(queue, plane, g0, g1):
            for q in range(4):
                queue.dma_start(
                    out=out_2[g0:g1, 4 * q:4 * q + 4, :].bitcast(I32).rearrange("g r m -> r g m"),
                    in_=plane[32 * q:32 * q + 4, :, :].bitcast(I32),
                )

        def turn_y(s):
            ya[s] = [psum.tile([P, 4, P], F32, name="ya") for i in range(TILES)]
            for i in range(TILES):
                for t in range(4):
                    nc.tensor.transpose(ya[s][i][:, t, :], yt[s][:, t, i * P:(i + 1) * P], ident[:])

        def store_y(s):
            h, g = divmod(s, GROUPS)
            dst = out_0[h * BLOCK:(h + 1) * BLOCK, g * GROUP:(g + 1) * GROUP].rearrange("(i b) n -> b i n", b=P)
            rows = work.tile([P, TILES, P, 4], F32, name="rows", align_bytes=256)
            for i in range(TILES):
                nc.scalar.copy(out=rows[:, i, :, :], in_=ya[s][i][:].rearrange("b t p -> b p t"))
            nc.sync.dma_start(out=dst, in_=rows[:].rearrange("b i p t -> b i (p t)"))

        def store_last(s):
            h, g = divmod(s, GROUPS)
            for i in range(TILES):
                rows = keep.tile([P, P, 4], F32, name="rows_last%d" % i)
                copy = nc.scalar.copy if i == 0 else nc.vector.tensor_copy
                copy(out=rows[:], in_=ya[s][i][:].rearrange("b t p -> b p t"))
                b0 = h * BLOCK + i * P
                queue = nc.scalar if i == 0 else nc.sync
                queue.dma_start(out=out_0[b0:b0 + P, g * GROUP:(g + 1) * GROUP], in_=rows[:].rearrange("b p t -> b (p t)"))

        turn_x(0)
        turn_x(1)
        scale_x(0)
        turn_x(2)
        quant_u(0)
        scale_x(1)
        quant_u(1)
        scale_x(2)
        quant_u(2)
        for n in range(GROUPS):
            sort_x(n)

        def turned_at(s):
            if s == 0:
                return list(range(GROUPS, 2 * GROUPS))
            return [s + GROUPS + 2] if 0 < s < STEPS - GROUPS - 2 else []

        for s in range(STEPS + 1):
            if s < STEPS:
                product(s)
            for n in turned_at(s - 1):
                scale_x(n)
            if s < STEPS:
                difference(s)
            for n in turned_at(s):
                sort_x(n)
            if s == 0:
                nc.scalar.activation(out=tau_neg[:], in_=tau_flat, func=ACT.Copy, scale=-1.0)
                nc.scalar.copy(out=tau_pos[:], in_=tau_flat)
            if s >= 1:
                turn_z(s - 1)
            if s >= 2:
                turn_y(s - 2)
            for n in turned_at(s):
                turn_x(n)
            if s == 1:
                for n in turned_at(s - 1):
                    quant_u(n)
            if s >= 1:
                threshold(s - 1)
            if s != 1:
                for n in turned_at(s - 1):
                    quant_u(n)
            if s >= 2:
                quant_y(s - 2)
            if s >= 1:
                round_y(s - 1)
            if s >= 2:
                store_y(s - 2)
        turn_y(STEPS - 1)
        store_last(STEPS - 1)
        quant_y(STEPS - 1)
